import numpy as np
import ml_dtypes


def mxq(x, axis, fmt="e4m3"):
    dtype, down = {"e4m3": (ml_dtypes.float8_e4m3fn, 7), "e5m2": (ml_dtypes.float8_e5m2, 14)}[fmt]
    v = np.moveaxis(np.asarray(x, np.float32).astype(ml_dtypes.bfloat16).astype(np.float64), axis, -1)
    blocks = v.reshape(v.shape[:-1] + (-1, 32))
    amax = np.abs(blocks).max(-1, keepdims=True)
    byte = np.maximum(np.where(amax > 0, np.frexp(amax)[1] - 1 + 127, 0) - down, 1)
    scale = np.exp2(byte - 127.0)
    codes = (blocks / scale).astype(np.float32).astype(dtype).astype(np.float64)
    return np.moveaxis((codes * scale).reshape(v.shape), -1, axis)


WIDE = False


def mx_kscale(k):
    if not WIDE:
        return np.ones(k)
    levels = np.array([30, -30])
    if k % 512:
        return np.exp2(np.random.permutation(np.resize(levels, k // 32))).repeat(32)
    a = np.empty((k // 512, 16))
    for p in range(k // 512):
        a[p, :8] = np.random.permutation(np.resize(levels, 8))
        for g in range(8):
            far = levels[np.abs(levels - a[p, g]) >= 10]
            a[p, g + 8] = far[np.random.randint(len(far))]
    return np.exp2(a.ravel()).repeat(32)


BF16 = ml_dtypes.bfloat16


def bf(x):
    return np.asarray(x, np.float32).astype(BF16)


def f64(x):
    return np.asarray(x).astype(np.float64)


E2M1 = np.array([0.0, 0.5, 1.0, 1.5, 2.0, 3.0, 4.0, 6.0, -0.0, -0.5, -1.0, -1.5, -2.0, -3.0, -4.0, -6.0])


def pack_weight(w, fmt):
    k, n = w.shape
    w = f64(bf(w)).reshape(k // 32, 32, n)
    amax = np.abs(w).max(1)
    if fmt == "e4m3":
        byte = np.frexp(amax)[1] - 1 + 127 - 7
    else:
        mant, ex = np.frexp(amax / 6.0)
        byte = np.where(mant > 0.5, ex, ex - 1) + 127
    byte = np.clip(np.where(amax > 0, byte, 1), 1, 254)
    scaled = (w * np.exp2(127.0 - byte)[:, None, :]).reshape(k, n).astype(np.float32)
    by_word = np.ascontiguousarray(scaled.reshape(k // 512, 128, 4, n).transpose(0, 1, 3, 2))
    if fmt == "e4m3":
        words = by_word.astype(ml_dtypes.float8_e4m3fn).view(np.uint8)
    else:
        c = by_word.astype(ml_dtypes.float4_e2m1fn).view(np.uint8) & 0xF
        words = c[..., 0::2] | (c[..., 1::2] << 4)
    return np.ascontiguousarray(words), np.ascontiguousarray(byte.astype(np.uint8).reshape(k // 512, 16, n))


def unpack_weight(words, scales, fmt):
    g, p, n, _ = words.shape
    if fmt == "e4m3":
        vals = np.ascontiguousarray(words).view(ml_dtypes.float8_e4m3fn).astype(np.float64)
    else:
        nib = np.empty((g, p, n, 4), np.uint8)
        nib[..., 0::2] = words & 0xF
        nib[..., 1::2] = words >> 4
        vals = E2M1[nib]
    vals = vals * np.repeat(np.exp2(scales.astype(np.float64) - 127.0), 8, axis=1)[..., None]
    return vals.transpose(0, 1, 3, 2).reshape(g * 512, n)
def pack4(w):
    words, scales = pack_weight(w, "e2m1")
    return words.reshape(words.shape[0], 128, -1), scales


def unpack4(words, scales):
    return unpack_weight(words.reshape(words.shape[0], 128, -1, 2), scales, "e2m1")


M, P, C, S = 1024, 1024, 2048, 512


def setup_inputs():
    s, t = mx_kscale(P), mx_kscale(C)
    orders = np.random.standard_normal((M, P)) * s
    inverse = np.random.standard_normal((P, C)) / np.sqrt(P) / s[:, None] * t
    stock = 0.5 * np.abs(np.random.standard_normal((M, C))) * t
    shares = 2.0 * np.random.standard_normal((C, S)) / np.sqrt(C) / t[:, None]
    contract = 0.3 * np.random.standard_normal(S)
    inv_words, inv_scales = pack4(inverse)
    return {"orders": bf(orders),
            "inv_words": inv_words,
            "inv_scales": inv_scales,
            "stock": bf(stock),
            "shares": bf(shares),
            "contract": bf(contract)}


def reference(orders, inv_words, inv_scales, stock, shares, contract):
    inverse = unpack4(inv_words, inv_scales)
    gross = mxq(f64(orders), 1, "e4m3") @ inverse
    net = np.maximum(gross - f64(stock), 0.0)
    load = mxq(net, 1, "e5m2") @ mxq(f64(shares), 0, "e4m3")
    return load + f64(contract)

@@ -1,0 +1,289 @@
+from contextlib import ExitStack
+
+import concourse.mybir as mybir
+from concourse.masks import make_identity
+
+M, K1, C, S = 1024, 1024, 2048, 512
+FLOPS = 2 * M * K1 * C + 2 * M * C * S
+
+F32 = mybir.dt.float32
+BF16 = mybir.dt.bfloat16
+I32 = mybir.dt.int32
+U32 = mybir.dt.uint32
+U8 = mybir.dt.uint8
+E4M3X4 = mybir.dt.float8_e4m3fn_x4
+E5M2X4 = mybir.dt.float8_e5m2_x4
+E2M1X4 = mybir.dt.float4_e2m1fn_x4
+SUB = mybir.AluOpType.subtract
+ADD = mybir.AluOpType.add
+MUL = mybir.AluOpType.mult
+RELU = mybir.ActivationFunctionType.Relu
+
+P = 128
+KP = 512
+MT = M // P
+G1 = K1 // KP
+G2 = C // KP
+N = 512
+LAG = 5
+
+
+def tile_material_requirements_planning_s9_kernel(tc, orders, inv_words, inv_scales, stock, shares, contract, out):
+    nc = tc.nc
+    with ExitStack() as ctx:
+        keep = ctx.enter_context(tc.tile_pool(name="keep", bufs=1))
+        work = ctx.enter_context(tc.tile_pool(name="work", bufs=3))
+        psum = ctx.enter_context(tc.psum_pool(name="psum", bufs=1))
+        ctx.enter_context(tc.manual_schedule())
+
+        ident = keep.tile([P, P], F32, name="ident")
+        dummy = keep.tile([P, 8], F32, name="dummy")
+        planes = keep.tile([P, G1, C], U8, name="planes", align_bytes=64)
+        inv_sb = [keep.tile([P, G1, 2 * N], U8, name="inv%d" % c, align_bytes=64) for c in range(G2)]
+        ord_sb = [keep.tile([P, K1], BF16, name="ord%d" % i, align_bytes=64) for i in range(MT)]
+        stk_sb = [keep.tile([P, C], BF16, name="stk%d" % i, align_bytes=64) for i in range(MT)]
+        sh_raw = [keep.tile([P, 4, S], BF16, name="shr%d" % g, align_bytes=64) for g in range(G2)]
+        sh_grp = [keep.tile([P, S, 4], BF16, name="shg%d" % g, align_bytes=64) for g in range(G2)]
+        sh_codes = [keep.tile([P, S], U32, name="shc%d" % g, align_bytes=64) for g in range(G2)]
+        sh_scales = [keep.tile([P, S], U8, name="shs%d" % g, align_bytes=64) for g in range(G2)]
+        ord_codes = [keep.tile([P, G1 * P], U32, name="oc%d" % i, align_bytes=64) for i in range(MT)]
+        ord_scales = [keep.tile([P, G1 * P], U8, name="os%d" % i, align_bytes=64) for i in range(MT)]
+        net_codes = [keep.tile([P, G2 * P], U32, name="nc%d" % i, align_bytes=64) for i in range(MT)]
+        net_scales = [keep.tile([P, G2 * P], U8, name="ns%d" % i, align_bytes=64) for i in range(MT)]
+        con_sb = keep.tile([P, S], BF16, name="con", align_bytes=64)
+
+        def load_orders(i):
+            nc.sync.dma_start(out=ord_sb[i][:], in_=orders[i * P : (i + 1) * P, :])
+
+        def load_stock(i, c0=0, c1=C):
+            nc.sync.dma_start(out=stk_sb[i][:, c0:c1], in_=stock[i * P : (i + 1) * P, c0:c1])
+
+        def load_inv(c):
+            nc.sync.dma_start(
+                out=inv_sb[c][:].bitcast(I32),
+                in_=inv_words.rearrange("g p b -> p g b")[:, :, 2 * N * c : 2 * N * (c + 1)].bitcast(I32),
+            )
+
+        def load_shares(g):
+            nc.sync.dma_start(out=sh_raw[g][:], in_=shares[g * KP : (g + 1) * KP, :].rearrange("(p j) s -> p j s", j=4))
+
+        nc.vector.memset(planes[:].rearrange("p g n -> p (g n)").bitcast(I32), 0)
+        nc.vector.memset(dummy[:], 0.0)
+        make_identity(nc, ident[:])
+        for r in range(4):
+            nc.scalar.dma_start(
+                out=planes[r:P:32, :, :].bitcast(I32),
+                in_=inv_scales.rearrange("g (q r) n -> r q g n", r=4)[r].bitcast(I32),
+            )
+        nc.scalar.activation(out=dummy[:], in_=dummy[:], func=RELU)
+
+        load_orders(0)
+        load_orders(1)
+        load_inv(0)
+        load_inv(1)
+        load_inv(2)
+        load_stock(0, 0, C // 2)
+        load_inv(3)
+        load_orders(2)
+        load_stock(0, C // 2, C)
+        load_stock(1)
+        load_shares(2)
+        load_orders(3)
+        load_stock(2)
+        load_shares(0)
+        load_orders(4)
+        load_shares(1)
+        load_stock(3)
+        load_shares(3)
+        load_orders(5)
+        load_stock(4)
+        load_orders(6)
+        load_stock(5)
+        load_orders(7)
+        load_stock(6)
+        load_stock(7)
+        nc.sync.dma_start(out=con_sb[:], in_=contract.partition_broadcast(P))
+
+        def bank(tag, bufs):
+            return psum.tile([P, N], F32, name=tag, tag=tag, bufs=bufs)
+
+        def turn_orders(i, g, t, slot, width):
+            words = ord_sb[i][:].bitcast(F32)
+            for u in range(2):
+                nc.tensor.transpose(t[:, u * width + slot * P : u * width + (slot + 1) * P], words[:, 256 * g + u : 256 * (g + 1) : 2], ident[:])
+
+        def orders_half(i, g, tag, bufs, engine_copy, grp):
+            t = bank(tag, bufs)
+            turn_orders(i, g, t, 0, P)
+            engine_copy(
+                out=grp[:, g * 512 : (g + 1) * 512].bitcast(F32).rearrange("p (x u) -> p x u", u=2),
+                in_=t[:, 0:256].rearrange("p (u x) -> p x u", u=2),
+            )
+
+        def orders_tile(i, tag, bufs, grp):
+            t = bank(tag, bufs)
+            for g in range(G1):
+                turn_orders(i, g, t, g, 2 * P)
+            nc.scalar.copy(
+                out=grp[:].bitcast(F32).rearrange("p (x u) -> p x u", u=2),
+                in_=t[:].rearrange("p (u x) -> p x u", u=2),
+            )
+
+        def quantize_orders(i, grp, a=0, b=G1):
+            nc.vector.quantize_mx(
+                out=ord_codes[i][:, a * P : b * P].bitcast(E4M3X4),
+                scales=ord_scales[i][:, a * P : b * P],
+                in_=grp[:, a * 512 : b * 512],
+            )
+
+        def first_product(i, c):
+            acc = bank("mm", 5)
+            for g in range(G1):
+                nc.tensor.matmul_mx(
+                    out=acc[:],
+                    lhsT=ord_codes[i][:, g * P : (g + 1) * P].bitcast(E4M3X4),
+                    lhsT_scale=ord_scales[i][:, g * P : (g + 1) * P],
+                    rhs=inv_sb[c][:, g, :].bitcast(E2M1X4),
+                    rhs_scale=planes[:, g, c * N : (c + 1) * N],
+                    start=(g == 0),
+                    stop=(g == G1 - 1),
+                )
+            return acc
+
+        def subtract_stock(i, c, acc, net):
+            nc.vector.tensor_tensor(
+                out=net[:, c * N : (c + 1) * N].rearrange("m (u p e) -> m u p e", u=2, e=2),
+                in0=acc[:].rearrange("m (p u e) -> m u p e", u=2, e=2),
+                in1=stk_sb[i][:, c * N : (c + 1) * N].rearrange("m (p u e) -> m u p e", u=2, e=2),
+                op=SUB,
+            )
+
+        def turn_net(net, h, tag, bufs):
+            t = bank(tag, bufs)
+            words = net[:].bitcast(F32)
+            for cl in range(2):
+                c = 2 * h + cl
+                for u in range(2):
+                    nc.tensor.transpose(t[:, u * 256 + cl * P : u * 256 + (cl + 1) * P], words[:, 256 * c + P * u : 256 * c + P * (u + 1)], ident[:])
+            return t
+
+        def relu_net(t, h, grp, on_vector=False):
+            o = grp[:, h * 1024 : (h + 1) * 1024].rearrange("p (x u e) -> p x u e", u=2, e=2)
+            i = t[:].bitcast(BF16).rearrange("p (u x e) -> p x u e", u=2, e=2)
+            if on_vector:
+                nc.vector.tensor_scalar_max(out=o, in0=i, scalar1=0.0)
+            else:
+                nc.scalar.activation(out=o, in_=i, func=RELU)
+
+        def quantize_net(i, grp, a=0, b=G2):
+            nc.vector.quantize_mx(
+                out=net_codes[i][:, a * P : b * P].bitcast(E5M2X4),
+                scales=net_scales[i][:, a * P : b * P],
+                in_=grp[:, a * 512 : b * 512],
+            )
+
+        def interleave_shares(g, s0, s1, engine):
+            o = sh_grp[g][:, s0:s1, :].rearrange("p (c i) t -> p c t i", i=4)
+            i = sh_raw[g][:, :, s0:s1].rearrange("p t (c i) -> p c t i", i=4)
+            if engine == "act":
+                nc.scalar.copy(out=o, in_=i)
+            else:
+                nc.gpsimd.tensor_scalar(out=sh_grp[g][:, s0:s1, :], in0=sh_raw[g][:, :, s0:s1].rearrange("p t c -> p c t"), scalar1=1.0, scalar2=0.0, op0=MUL, op1=ADD)
+
+        def quantize_shares(g):
+            nc.vector.quantize_mx(out=sh_codes[g][:].bitcast(E4M3X4), scales=sh_scales[g][:], in_=sh_grp[g][:].rearrange("p s t -> p (s t)"))
+
+        def second_product(i):
+            acc = bank("mm", 5)
+            for n, g in enumerate((2, 0, 3, 1)):
+                nc.tensor.matmul_mx(
+                    out=acc[:],
+                    lhsT=net_codes[i][:, g * P : (g + 1) * P].bitcast(E5M2X4),
+                    lhsT_scale=net_scales[i][:, g * P : (g + 1) * P],
+                    rhs=sh_codes[g][:].bitcast(E4M3X4),
+                    rhs_scale=sh_scales[g][:],
+                    start=(n == 0),
+                    stop=(n == G2 - 1),
+                )
+            return acc
+
+        def add_and_store(i, acc, parts=1):
+            res = work.tile([P, S], F32, name="res", bufs=4)
+            w = S // parts
+            for k in range(parts):
+                nc.vector.tensor_tensor(out=res[:, k * w : (k + 1) * w], in0=acc[:, k * w : (k + 1) * w], in1=con_sb[:, k * w : (k + 1) * w], op=ADD)
+                queue = nc.sync if k % 2 == 0 else nc.scalar
+                queue.dma_start(out=out[i * P : (i + 1) * P, k * w : (k + 1) * w], in_=res[:, k * w : (k + 1) * w])
+
+        og = {}
+        nets = {}
+        ng = {}
+        for i in range(MT):
+            og[i] = work.tile([P, K1], BF16, name="og", align_bytes=64) if i < 2 else None
+        orders_half(0, 0, "ot", 1, nc.scalar.copy, og[0])
+        orders_half(0, 1, "nt", 2, nc.vector.tensor_copy, og[0])
+        quantize_orders(0, og[0], 0, 1)
+        quantize_orders(0, og[0], 1, 2)
+        orders_tile(1, "nt", 2, og[1])
+
+        for i in range(MT):
+            if i >= 3:
+                quantize_net(i - 3, ng[i - 3])
+            if i + 1 < MT:
+                quantize_orders(i + 1, og[i + 1])
+            nets[i] = work.tile([P, C], BF16, name="net", align_bytes=64)
+            for c in range(G2):
+                acc = first_product(i, c)
+                subtract_stock(i, c, acc, nets[i])
+            if i >= LAG:
+                acc = second_product(i - LAG)
+            if i + 2 < MT:
+                og[i + 2] = work.tile([P, K1], BF16, name="og", align_bytes=64)
+                orders_tile(i + 2, "ot", 1, og[i + 2])
+            if i >= 1:
+                ng[i - 1] = work.tile([P, C], BF16, name="ng", align_bytes=64)
+                for h in range(2):
+                    t = turn_net(nets[i - 1], h, "nt", 2)
+                    relu_net(t, h, ng[i - 1])
+            if i == 0:
+                for q in range(4):
+                    interleave_shares(2, q * 128, (q + 1) * 128, "pool")
+            if i in (1, 2):
+                interleave_shares(0, (i - 1) * 256, i * 256, "act")
+            if i == 2:
+                for q in range(4):
+                    interleave_shares(3, q * 128, (q + 1) * 128, "pool")
+            if i in (3, 4):
+                interleave_shares(1, (i - 3) * 256, (i - 2) * 256, "act")
+            if i == 2:
+                quantize_shares(2)
+            if i == 3:
+                quantize_shares(0)
+            if i == 4:
+                quantize_shares(3)
+                quantize_shares(1)
+            if i >= LAG:
+                if i < MT - 1:
+                    add_and_store(i - LAG, acc)
+                else:
+                    quantize_net(5, ng[5])
+                    add_and_store(i - LAG, acc)
+
+        acc3 = second_product(3)
+        acc4 = second_product(4)
+        ng[7] = work.tile([P, C], BF16, name="ng", align_bytes=64)
+        t0 = turn_net(nets[7], 0, "mm", 5)
+        t1 = turn_net(nets[7], 1, "mm", 5)
+        add_and_store(3, acc3)
+        quantize_net(6, ng[6])
+        relu_net(t0, 0, ng[7])
+        relu_net(t1, 1, ng[7], on_vector=True)
+        add_and_store(4, acc4)
+        quantize_net(7, ng[7], 0, 2)
+        quantize_net(7, ng[7], 2, 4)
+        acc5 = second_product(5)
+        acc6 = second_product(6)
+        acc7 = second_product(7)
+        add_and_store(5, acc5)
+        add_and_store(6, acc6)
+        add_and_store(7, acc7, parts=2)

@@ -25,7 +25,9 @@ MT = M // P
 G1 = K1 // KP
 G2 = C // KP
 N = 512
-LAG = 5
+TO2X, TO2C, QO2X, QO2C = 1, 1, 1, 2
+S2_AFTER = {6: (0, 1, 2), 7: (3,)}
+VECTOR_RELU = {(0, 0), (1, 0), (2, 0), (3, 0), (6, 1)}
 
 
 def tile_material_requirements_planning_s9_kernel(tc, orders, inv_words, inv_scales, stock, shares, contract, out):
@@ -70,34 +72,36 @@ def tile_material_requirements_planning_s9_kernel(tc, orders, inv_words, inv_sca
         nc.vector.memset(planes[:].rearrange("p g n -> p (g n)").bitcast(I32), 0)
         nc.vector.memset(dummy[:], 0.0)
         make_identity(nc, ident[:])
+        nc.scalar.activation(out=dummy[:], in_=dummy[:], func=RELU)
+
+        for g in range(G1):
+            nc.sync.dma_start(out=ord_sb[0][:, g * KP : (g + 1) * KP], in_=orders[0:P, g * KP : (g + 1) * KP])
         for r in range(4):
-            nc.scalar.dma_start(
+            nc.sync.dma_start(
                 out=planes[r:P:32, :, :].bitcast(I32),
                 in_=inv_scales.rearrange("g (q r) n -> r q g n", r=4)[r].bitcast(I32),
             )
-        nc.scalar.activation(out=dummy[:], in_=dummy[:], func=RELU)
-
-        load_orders(0)
         load_orders(1)
         load_inv(0)
-        load_inv(1)
-        load_inv(2)
         load_stock(0, 0, C // 2)
-        load_inv(3)
+        load_inv(1)
+        load_stock(1, 0, C // 2)
+        load_inv(2)
         load_orders(2)
         load_stock(0, C // 2, C)
-        load_stock(1)
-        load_shares(2)
+        load_inv(3)
+        load_stock(1, C // 2, C)
         load_orders(3)
-        load_stock(2)
         load_shares(0)
+        load_stock(2)
         load_orders(4)
         load_shares(1)
         load_stock(3)
-        load_shares(3)
         load_orders(5)
+        load_shares(2)
         load_stock(4)
         load_orders(6)
+        load_shares(3)
         load_stock(5)
         load_orders(7)
         load_stock(6)
@@ -195,7 +199,7 @@ def tile_material_requirements_planning_s9_kernel(tc, orders, inv_words, inv_sca
 
         def second_product(i):
             acc = bank("mm", 5)
-            for n, g in enumerate((2, 0, 3, 1)):
+            for n, g in enumerate(range(G2)):
                 nc.tensor.matmul_mx(
                     out=acc[:],
                     lhsT=net_codes[i][:, g * P : (g + 1) * P].bitcast(E5M2X4),
@@ -215,75 +219,62 @@ def tile_material_requirements_planning_s9_kernel(tc, orders, inv_words, inv_sca
                 queue = nc.sync if k % 2 == 0 else nc.scalar
                 queue.dma_start(out=out[i * P : (i + 1) * P, k * w : (k + 1) * w], in_=res[:, k * w : (k + 1) * w])
 
-        og = {}
-        nets = {}
-        ng = {}
-        for i in range(MT):
-            og[i] = work.tile([P, K1], BF16, name="og", align_bytes=64) if i < 2 else None
-        orders_half(0, 0, "ot", 1, nc.scalar.copy, og[0])
+        og, nets, ng = {}, {}, {}
+
+        def new_og(i):
+            og[i] = work.tile([P, K1], BF16, name="og", align_bytes=64)
+            return og[i]
+
+        new_og(0)
+        orders_half(0, 0, "nt", 2, nc.scalar.copy, og[0])
         orders_half(0, 1, "nt", 2, nc.vector.tensor_copy, og[0])
         quantize_orders(0, og[0], 0, 1)
         quantize_orders(0, og[0], 1, 2)
-        orders_tile(1, "nt", 2, og[1])
+        orders_tile(1, "ot", 1, new_og(1))
+        quantize_orders(1, og[1])
 
-        for i in range(MT):
-            if i >= 3:
-                quantize_net(i - 3, ng[i - 3])
-            if i + 1 < MT:
-                quantize_orders(i + 1, og[i + 1])
-            nets[i] = work.tile([P, C], BF16, name="net", align_bytes=64)
+        for tiles in ((0, 1), (2,), (3,), (4,), (5,), (6,), (7,)):
+            i = tiles[-1]
+            for x in tiles:
+                nets[x] = work.tile([P, C], BF16, name="net", align_bytes=64)
             for c in range(G2):
-                acc = first_product(i, c)
-                subtract_stock(i, c, acc, nets[i])
-            if i >= LAG:
-                acc = second_product(i - LAG)
+                for x in tiles:
+                    acc = first_product(x, c)
+                    if x == TO2X and c == TO2C:
+                        orders_tile(2, "ot", 1, new_og(2))
+                    if c == 3 and x >= 3:
+                        quantize_net(x - 3, ng[x - 3])
+                    subtract_stock(x, c, acc, nets[x])
+                    if x == QO2X and c == QO2C:
+                        quantize_orders(2, og[2])
+                    if c == 0 and 2 <= x < MT - 1:
+                        quantize_orders(x + 1, og[x + 1])
+            if 2 <= i < 6:
+                quantize_shares(i - 2)
+            accs = [(n, second_product(n)) for n in S2_AFTER.get(i, ())]
             if i + 2 < MT:
-                og[i + 2] = work.tile([P, K1], BF16, name="og", align_bytes=64)
-                orders_tile(i + 2, "ot", 1, og[i + 2])
+                orders_tile(i + 2, "ot", 1, new_og(i + 2))
             if i >= 1:
                 ng[i - 1] = work.tile([P, C], BF16, name="ng", align_bytes=64)
                 for h in range(2):
                     t = turn_net(nets[i - 1], h, "nt", 2)
-                    relu_net(t, h, ng[i - 1])
-            if i == 0:
-                for q in range(4):
-                    interleave_shares(2, q * 128, (q + 1) * 128, "pool")
-            if i in (1, 2):
-                interleave_shares(0, (i - 1) * 256, i * 256, "act")
-            if i == 2:
-                for q in range(4):
-                    interleave_shares(3, q * 128, (q + 1) * 128, "pool")
-            if i in (3, 4):
-                interleave_shares(1, (i - 3) * 256, (i - 2) * 256, "act")
-            if i == 2:
-                quantize_shares(2)
-            if i == 3:
-                quantize_shares(0)
-            if i == 4:
-                quantize_shares(3)
-                quantize_shares(1)
-            if i >= LAG:
-                if i < MT - 1:
-                    add_and_store(i - LAG, acc)
-                else:
-                    quantize_net(5, ng[5])
-                    add_and_store(i - LAG, acc)
+                    relu_net(t, h, ng[i - 1], on_vector=(i - 1, h) in VECTOR_RELU)
+            if 1 <= i <= 4:
+                interleave_shares(i - 1, 0, S // 2, "act")
+                interleave_shares(i - 1, S // 2, S, "act")
+            if i == MT - 1:
+                quantize_net(5, ng[5])
+            for n, acc in accs:
+                add_and_store(n, acc)
 
-        acc3 = second_product(3)
-        acc4 = second_product(4)
         ng[7] = work.tile([P, C], BF16, name="ng", align_bytes=64)
         t0 = turn_net(nets[7], 0, "mm", 5)
         t1 = turn_net(nets[7], 1, "mm", 5)
-        add_and_store(3, acc3)
         quantize_net(6, ng[6])
         relu_net(t0, 0, ng[7])
         relu_net(t1, 1, ng[7], on_vector=True)
-        add_and_store(4, acc4)
         quantize_net(7, ng[7], 0, 2)
         quantize_net(7, ng[7], 2, 4)
-        acc5 = second_product(5)
-        acc6 = second_product(6)
-        acc7 = second_product(7)
-        add_and_store(5, acc5)
-        add_and_store(6, acc6)
-        add_and_store(7, acc7, parts=2)
+        accs = [(n, second_product(n)) for n in (4, 5, 6, 7)]
+        for n, acc in accs:
+            add_and_store(n, acc, parts=2 if n == MT - 1 else 1)

@@ -16,7 +16,6 @@ E5M2X4 = mybir.dt.float8_e5m2_x4
 E2M1X4 = mybir.dt.float4_e2m1fn_x4
 SUB = mybir.AluOpType.subtract
 ADD = mybir.AluOpType.add
-MUL = mybir.AluOpType.mult
 RELU = mybir.ActivationFunctionType.Relu
 
 P = 128
@@ -25,9 +24,8 @@ MT = M // P
 G1 = K1 // KP
 G2 = C // KP
 N = 512
-TO2X, TO2C, QO2X, QO2C = 1, 1, 1, 2
-S2_AFTER = {6: (0, 1, 2), 7: (3,)}
-VECTOR_RELU = {(0, 0), (1, 0), (2, 0), (3, 0), (6, 1)}
+QS_AFTER = {1: 0, 3: 1, 5: 2, 6: 3}
+SI_AFTER = {1: (1, 0), 2: (1, 1), 4: (3, 0), 5: (3, 1)}
 
 
 def tile_material_requirements_planning_s9_kernel(tc, orders, inv_words, inv_scales, stock, shares, contract, out):
@@ -85,23 +83,23 @@ def tile_material_requirements_planning_s9_kernel(tc, orders, inv_words, inv_sca
         load_inv(0)
         load_stock(0, 0, C // 2)
         load_inv(1)
+        load_orders(2)
         load_stock(1, 0, C // 2)
         load_inv(2)
-        load_orders(2)
         load_stock(0, C // 2, C)
         load_inv(3)
         load_stock(1, C // 2, C)
-        load_orders(3)
         load_shares(0)
+        load_orders(3)
         load_stock(2)
-        load_orders(4)
         load_shares(1)
+        load_orders(4)
         load_stock(3)
-        load_orders(5)
         load_shares(2)
+        load_orders(5)
         load_stock(4)
-        load_orders(6)
         load_shares(3)
+        load_orders(6)
         load_stock(5)
         load_orders(7)
         load_stock(6)
@@ -192,7 +190,7 @@ def tile_material_requirements_planning_s9_kernel(tc, orders, inv_words, inv_sca
             if engine == "act":
                 nc.scalar.copy(out=o, in_=i)
             else:
-                nc.gpsimd.tensor_scalar(out=sh_grp[g][:, s0:s1, :], in0=sh_raw[g][:, :, s0:s1].rearrange("p t c -> p c t"), scalar1=1.0, scalar2=0.0, op0=MUL, op1=ADD)
+                nc.vector.tensor_copy(out=o, in_=i)
 
         def quantize_shares(g):
             nc.vector.quantize_mx(out=sh_codes[g][:].bitcast(E4M3X4), scales=sh_scales[g][:], in_=sh_grp[g][:].rearrange("p s t -> p (s t)"))
@@ -240,41 +238,50 @@ def tile_material_requirements_planning_s9_kernel(tc, orders, inv_words, inv_sca
             for c in range(G2):
                 for x in tiles:
                     acc = first_product(x, c)
-                    if x == TO2X and c == TO2C:
+                    if x == 1 and c == 0:
                         orders_tile(2, "ot", 1, new_og(2))
-                    if c == 3 and x >= 3:
-                        quantize_net(x - 3, ng[x - 3])
+                        interleave_shares(0, 0, S // 2, "act")
+                        interleave_shares(0, S // 2, S, "act")
+                    if c == 2 and x >= 4:
+                        quantize_net(x - 4, ng[x - 4])
                     subtract_stock(x, c, acc, nets[x])
-                    if x == QO2X and c == QO2C:
+                    if x == 1 and c == 1:
                         quantize_orders(2, og[2])
                     if c == 0 and 2 <= x < MT - 1:
                         quantize_orders(x + 1, og[x + 1])
-            if 2 <= i < 6:
-                quantize_shares(i - 2)
-            accs = [(n, second_product(n)) for n in S2_AFTER.get(i, ())]
+                if i == 4 and c == 1:
+                    interleave_shares(2, S // 2, S, "dve")
+            if i == 3:
+                interleave_shares(2, 0, S // 2, "dve")
+            if i in QS_AFTER:
+                quantize_shares(QS_AFTER[i])
+            accs = [(n, second_product(n)) for n in (range(3) if i == MT - 1 else ())]
             if i + 2 < MT:
                 orders_tile(i + 2, "ot", 1, new_og(i + 2))
-            if i >= 1:
-                ng[i - 1] = work.tile([P, C], BF16, name="ng", align_bytes=64)
-                for h in range(2):
-                    t = turn_net(nets[i - 1], h, "nt", 2)
-                    relu_net(t, h, ng[i - 1], on_vector=(i - 1, h) in VECTOR_RELU)
-            if 1 <= i <= 4:
-                interleave_shares(i - 1, 0, S // 2, "act")
-                interleave_shares(i - 1, S // 2, S, "act")
-            if i == MT - 1:
-                quantize_net(5, ng[5])
-            for n, acc in accs:
-                add_and_store(n, acc)
+            ng[i - 1] = work.tile([P, C], BF16, name="ng", align_bytes=64, bufs=5)
+            for h in range(2):
+                t = turn_net(nets[i - 1], h, "nt", 2)
+                relu_net(t, h, ng[i - 1], on_vector=(i == 1 and h == 0))
+            if i in SI_AFTER:
+                g, h = SI_AFTER[i]
+                interleave_shares(g, h * S // 2, (h + 1) * S // 2, "act")
+        quantize_net(4, ng[4])
+        quantize_net(5, ng[5])
+        for n, acc in accs:
+            add_and_store(n, acc)
 
-        ng[7] = work.tile([P, C], BF16, name="ng", align_bytes=64)
+        acc3 = second_product(3)
+        acc4 = second_product(4)
+        ng[7] = work.tile([P, C], BF16, name="ng", align_bytes=64, bufs=5)
         t0 = turn_net(nets[7], 0, "mm", 5)
         t1 = turn_net(nets[7], 1, "mm", 5)
+        add_and_store(3, acc3)
         quantize_net(6, ng[6])
         relu_net(t0, 0, ng[7])
         relu_net(t1, 1, ng[7], on_vector=True)
+        add_and_store(4, acc4)
         quantize_net(7, ng[7], 0, 2)
         quantize_net(7, ng[7], 2, 4)
-        accs = [(n, second_product(n)) for n in (4, 5, 6, 7)]
+        accs = [(n, second_product(n)) for n in (5, 6, 7)]
         for n, acc in accs:
             add_and_store(n, acc, parts=2 if n == MT - 1 else 1)

from contextlib import ExitStack

import concourse.mybir as mybir
from concourse.masks import make_identity

M, K1, C, S = 1024, 1024, 2048, 512
FLOPS = 2 * M * K1 * C + 2 * M * C * S

F32 = mybir.dt.float32
BF16 = mybir.dt.bfloat16
I32 = mybir.dt.int32
U32 = mybir.dt.uint32
U8 = mybir.dt.uint8
E4M3X4 = mybir.dt.float8_e4m3fn_x4
E5M2X4 = mybir.dt.float8_e5m2_x4
E2M1X4 = mybir.dt.float4_e2m1fn_x4
SUB = mybir.AluOpType.subtract
ADD = mybir.AluOpType.add
RELU = mybir.ActivationFunctionType.Relu

P = 128
KP = 512
MT = M // P
G1 = K1 // KP
G2 = C // KP
N = 512
QS_AFTER = {1: 0, 3: 1, 5: 2, 6: 3}
SI_AFTER = {1: (1, 0), 2: (1, 1), 4: (3, 0), 5: (3, 1)}


def tile_material_requirements_planning_s9_kernel(tc, orders, inv_words, inv_scales, stock, shares, contract, out):
    nc = tc.nc
    with ExitStack() as ctx:
        keep = ctx.enter_context(tc.tile_pool(name="keep", bufs=1))
        work = ctx.enter_context(tc.tile_pool(name="work", bufs=3))
        psum = ctx.enter_context(tc.psum_pool(name="psum", bufs=1))
        ctx.enter_context(tc.manual_schedule())

        ident = keep.tile([P, P], F32, name="ident")
        dummy = keep.tile([P, 8], F32, name="dummy")
        planes = keep.tile([P, G1, C], U8, name="planes", align_bytes=64)
        inv_sb = [keep.tile([P, G1, 2 * N], U8, name="inv%d" % c, align_bytes=64) for c in range(G2)]
        ord_sb = [keep.tile([P, K1], BF16, name="ord%d" % i, align_bytes=64) for i in range(MT)]
        stk_sb = [keep.tile([P, C], BF16, name="stk%d" % i, align_bytes=64) for i in range(MT)]
        sh_raw = [keep.tile([P, 4, S], BF16, name="shr%d" % g, align_bytes=64) for g in range(G2)]
        sh_grp = [keep.tile([P, S, 4], BF16, name="shg%d" % g, align_bytes=64) for g in range(G2)]
        sh_codes = [keep.tile([P, S], U32, name="shc%d" % g, align_bytes=64) for g in range(G2)]
        sh_scales = [keep.tile([P, S], U8, name="shs%d" % g, align_bytes=64) for g in range(G2)]
        ord_codes = [keep.tile([P, G1 * P], U32, name="oc%d" % i, align_bytes=64) for i in range(MT)]
        ord_scales = [keep.tile([P, G1 * P], U8, name="os%d" % i, align_bytes=64) for i in range(MT)]
        net_codes = [keep.tile([P, G2 * P], U32, name="nc%d" % i, align_bytes=64) for i in range(MT)]
        net_scales = [keep.tile([P, G2 * P], U8, name="ns%d" % i, align_bytes=64) for i in range(MT)]
        con_sb = keep.tile([P, S], BF16, name="con", align_bytes=64)

        def load_orders(i):
            nc.sync.dma_start(out=ord_sb[i][:], in_=orders[i * P : (i + 1) * P, :])

        def load_stock(i, c0=0, c1=C):
            nc.sync.dma_start(out=stk_sb[i][:, c0:c1], in_=stock[i * P : (i + 1) * P, c0:c1])

        def load_inv(c):
            nc.sync.dma_start(
                out=inv_sb[c][:].bitcast(I32),
                in_=inv_words.rearrange("g p b -> p g b")[:, :, 2 * N * c : 2 * N * (c + 1)].bitcast(I32),
            )

        def load_shares(g):
            nc.sync.dma_start(out=sh_raw[g][:], in_=shares[g * KP : (g + 1) * KP, :].rearrange("(p j) s -> p j s", j=4))

        nc.vector.memset(planes[:].rearrange("p g n -> p (g n)").bitcast(I32), 0)
        nc.vector.memset(dummy[:], 0.0)
        make_identity(nc, ident[:])
        nc.scalar.activation(out=dummy[:], in_=dummy[:], func=RELU)

        for g in range(G1):
            nc.sync.dma_start(out=ord_sb[0][:, g * KP : (g + 1) * KP], in_=orders[0:P, g * KP : (g + 1) * KP])
        for r in range(4):
            nc.sync.dma_start(
                out=planes[r:P:32, :, :].bitcast(I32),
                in_=inv_scales.rearrange("g (q r) n -> r q g n", r=4)[r].bitcast(I32),
            )
        load_orders(1)
        load_inv(0)
        load_stock(0, 0, C // 2)
        load_inv(1)
        load_orders(2)
        load_stock(1, 0, C // 2)
        load_inv(2)
        load_stock(0, C // 2, C)
        load_inv(3)
        load_stock(1, C // 2, C)
        load_shares(0)
        load_orders(3)
        load_stock(2)
        load_shares(1)
        load_orders(4)
        load_stock(3)
        load_shares(2)
        load_orders(5)
        load_stock(4)
        load_shares(3)
        load_orders(6)
        load_stock(5)
        load_orders(7)
        load_stock(6)
        load_stock(7)
        nc.sync.dma_start(out=con_sb[:], in_=contract.partition_broadcast(P))

        def bank(tag, bufs):
            return psum.tile([P, N], F32, name=tag, tag=tag, bufs=bufs)

        def turn_orders(i, g, t, slot, width):
            words = ord_sb[i][:].bitcast(F32)
            for u in range(2):
                nc.tensor.transpose(t[:, u * width + slot * P : u * width + (slot + 1) * P], words[:, 256 * g + u : 256 * (g + 1) : 2], ident[:])

        def orders_half(i, g, tag, bufs, engine_copy, grp):
            t = bank(tag, bufs)
            turn_orders(i, g, t, 0, P)
            engine_copy(
                out=grp[:, g * 512 : (g + 1) * 512].bitcast(F32).rearrange("p (x u) -> p x u", u=2),
                in_=t[:, 0:256].rearrange("p (u x) -> p x u", u=2),
            )

        def orders_tile(i, tag, bufs, grp):
            t = bank(tag, bufs)
            for g in range(G1):
                turn_orders(i, g, t, g, 2 * P)
            nc.scalar.copy(
                out=grp[:].bitcast(F32).rearrange("p (x u) -> p x u", u=2),
                in_=t[:].rearrange("p (u x) -> p x u", u=2),
            )

        def quantize_orders(i, grp, a=0, b=G1):
            nc.vector.quantize_mx(
                out=ord_codes[i][:, a * P : b * P].bitcast(E4M3X4),
                scales=ord_scales[i][:, a * P : b * P],
                in_=grp[:, a * 512 : b * 512],
            )

        def first_product(i, c):
            acc = bank("mm", 5)
            for g in range(G1):
                nc.tensor.matmul_mx(
                    out=acc[:],
                    lhsT=ord_codes[i][:, g * P : (g + 1) * P].bitcast(E4M3X4),
                    lhsT_scale=ord_scales[i][:, g * P : (g + 1) * P],
                    rhs=inv_sb[c][:, g, :].bitcast(E2M1X4),
                    rhs_scale=planes[:, g, c * N : (c + 1) * N],
                    start=(g == 0),
                    stop=(g == G1 - 1),
                )
            return acc

        def subtract_stock(i, c, acc, net):
            nc.vector.tensor_tensor(
                out=net[:, c * N : (c + 1) * N].rearrange("m (u p e) -> m u p e", u=2, e=2),
                in0=acc[:].rearrange("m (p u e) -> m u p e", u=2, e=2),
                in1=stk_sb[i][:, c * N : (c + 1) * N].rearrange("m (p u e) -> m u p e", u=2, e=2),
                op=SUB,
            )

        def turn_net(net, h, tag, bufs):
            t = bank(tag, bufs)
            words = net[:].bitcast(F32)
            for cl in range(2):
                c = 2 * h + cl
                for u in range(2):
                    nc.tensor.transpose(t[:, u * 256 + cl * P : u * 256 + (cl + 1) * P], words[:, 256 * c + P * u : 256 * c + P * (u + 1)], ident[:])
            return t

        def relu_net(t, h, grp, on_vector=False):
            o = grp[:, h * 1024 : (h + 1) * 1024].rearrange("p (x u e) -> p x u e", u=2, e=2)
            i = t[:].bitcast(BF16).rearrange("p (u x e) -> p x u e", u=2, e=2)
            if on_vector:
                nc.vector.tensor_scalar_max(out=o, in0=i, scalar1=0.0)
            else:
                nc.scalar.activation(out=o, in_=i, func=RELU)

        def quantize_net(i, grp, a=0, b=G2):
            nc.vector.quantize_mx(
                out=net_codes[i][:, a * P : b * P].bitcast(E5M2X4),
                scales=net_scales[i][:, a * P : b * P],
                in_=grp[:, a * 512 : b * 512],
            )

        def interleave_shares(g, s0, s1, engine):
            o = sh_grp[g][:, s0:s1, :].rearrange("p (c i) t -> p c t i", i=4)
            i = sh_raw[g][:, :, s0:s1].rearrange("p t (c i) -> p c t i", i=4)
            if engine == "act":
                nc.scalar.copy(out=o, in_=i)
            else:
                nc.vector.tensor_copy(out=o, in_=i)

        def quantize_shares(g):
            nc.vector.quantize_mx(out=sh_codes[g][:].bitcast(E4M3X4), scales=sh_scales[g][:], in_=sh_grp[g][:].rearrange("p s t -> p (s t)"))

        def second_product(i):
            acc = bank("mm", 5)
            for n, g in enumerate(range(G2)):
                nc.tensor.matmul_mx(
                    out=acc[:],
                    lhsT=net_codes[i][:, g * P : (g + 1) * P].bitcast(E5M2X4),
                    lhsT_scale=net_scales[i][:, g * P : (g + 1) * P],
                    rhs=sh_codes[g][:].bitcast(E4M3X4),
                    rhs_scale=sh_scales[g][:],
                    start=(n == 0),
                    stop=(n == G2 - 1),
                )
            return acc

        def add_and_store(i, acc, parts=1):
            res = work.tile([P, S], F32, name="res", bufs=4)
            w = S // parts
            for k in range(parts):
                nc.vector.tensor_tensor(out=res[:, k * w : (k + 1) * w], in0=acc[:, k * w : (k + 1) * w], in1=con_sb[:, k * w : (k + 1) * w], op=ADD)
                queue = nc.sync if k % 2 == 0 else nc.scalar
                queue.dma_start(out=out[i * P : (i + 1) * P, k * w : (k + 1) * w], in_=res[:, k * w : (k + 1) * w])

        og, nets, ng = {}, {}, {}

        def new_og(i):
            og[i] = work.tile([P, K1], BF16, name="og", align_bytes=64)
            return og[i]

        new_og(0)
        orders_half(0, 0, "nt", 2, nc.scalar.copy, og[0])
        orders_half(0, 1, "nt", 2, nc.vector.tensor_copy, og[0])
        quantize_orders(0, og[0], 0, 1)
        quantize_orders(0, og[0], 1, 2)
        orders_tile(1, "ot", 1, new_og(1))
        quantize_orders(1, og[1])

        for tiles in ((0, 1), (2,), (3,), (4,), (5,), (6,), (7,)):
            i = tiles[-1]
            for x in tiles:
                nets[x] = work.tile([P, C], BF16, name="net", align_bytes=64)
            for c in range(G2):
                for x in tiles:
                    acc = first_product(x, c)
                    if x == 1 and c == 0:
                        orders_tile(2, "ot", 1, new_og(2))
                        interleave_shares(0, 0, S // 2, "act")
                        interleave_shares(0, S // 2, S, "act")
                    if c == 2 and x >= 4:
                        quantize_net(x - 4, ng[x - 4])
                    subtract_stock(x, c, acc, nets[x])
                    if x == 1 and c == 1:
                        quantize_orders(2, og[2])
                    if c == 0 and 2 <= x < MT - 1:
                        quantize_orders(x + 1, og[x + 1])
                if i == 4 and c == 1:
                    interleave_shares(2, S // 2, S, "dve")
            if i == 3:
                interleave_shares(2, 0, S // 2, "dve")
            if i in QS_AFTER:
                quantize_shares(QS_AFTER[i])
            accs = [(n, second_product(n)) for n in (range(3) if i == MT - 1 else ())]
            if i + 2 < MT:
                orders_tile(i + 2, "ot", 1, new_og(i + 2))
            ng[i - 1] = work.tile([P, C], BF16, name="ng", align_bytes=64, bufs=5)
            for h in range(2):
                t = turn_net(nets[i - 1], h, "nt", 2)
                relu_net(t, h, ng[i - 1], on_vector=(i == 1 and h == 0))
            if i in SI_AFTER:
                g, h = SI_AFTER[i]
                interleave_shares(g, h * S // 2, (h + 1) * S // 2, "act")
        quantize_net(4, ng[4])
        quantize_net(5, ng[5])
        for n, acc in accs:
            add_and_store(n, acc)

        acc3 = second_product(3)
        acc4 = second_product(4)
        ng[7] = work.tile([P, C], BF16, name="ng", align_bytes=64, bufs=5)
        t0 = turn_net(nets[7], 0, "mm", 5)
        t1 = turn_net(nets[7], 1, "mm", 5)
        add_and_store(3, acc3)
        quantize_net(6, ng[6])
        relu_net(t0, 0, ng[7])
        relu_net(t1, 1, ng[7], on_vector=True)
        add_and_store(4, acc4)
        quantize_net(7, ng[7], 0, 2)
        quantize_net(7, ng[7], 2, 4)
        accs = [(n, second_product(n)) for n in (5, 6, 7)]
        for n, acc in accs:
            add_and_store(n, acc, parts=2 if n == MT - 1 else 1)
